import numpy as np
import ml_dtypes


def mxq(x, axis, fmt="e4m3"):
    dtype, down = {"e4m3": (ml_dtypes.float8_e4m3fn, 7), "e5m2": (ml_dtypes.float8_e5m2, 14)}[fmt]
    v = np.moveaxis(np.asarray(x, np.float32).astype(ml_dtypes.bfloat16).astype(np.float64), axis, -1)
    blocks = v.reshape(v.shape[:-1] + (-1, 32))
    amax = np.abs(blocks).max(-1, keepdims=True)
    byte = np.maximum(np.where(amax > 0, np.frexp(amax)[1] - 1 + 127, 0) - down, 1)
    scale = np.exp2(byte - 127.0)
    codes = (blocks / scale).astype(np.float32).astype(dtype).astype(np.float64)
    return np.moveaxis((codes * scale).reshape(v.shape), -1, axis)


WIDE = False


def mx_kscale(k):
    if not WIDE:
        return np.ones(k)
    levels = np.array([10, -10, 5, -5, 0])
    if k % 512:
        return np.exp2(np.random.permutation(np.resize(levels, k // 32))).repeat(32)
    a = np.empty((k // 512, 16))
    for p in range(k // 512):
        a[p, :8] = np.random.permutation(np.resize(levels, 8))
        for g in range(8):
            far = levels[np.abs(levels - a[p, g]) >= 10]
            a[p, g + 8] = far[np.random.randint(len(far))]
    return np.exp2(a.ravel()).repeat(32)


def f64(x):
    return np.asarray(x).astype(np.float64)


def striped8(idx):
    return np.asarray(idx).reshape(8, -1, 16).transpose(0, 2, 1).reshape(128, -1).astype(np.uint16)


def unstriped8(offs):
    return offs.reshape(8, 16, -1).transpose(0, 2, 1).reshape(8, -1).astype(np.int64)


def pick8(x, idx, run):
    r = np.arange(len(x))
    return x[r[:, None], idx[r % (8 * run) // run]]


E2M1 = np.array([0.0, 0.5, 1.0, 1.5, 2.0, 3.0, 4.0, 6.0, -0.0, -0.5, -1.0, -1.5, -2.0, -3.0, -4.0, -6.0])


def pack_weight(w, fmt):
    k, n = w.shape
    w = f64(np.asarray(w, np.float32).astype(ml_dtypes.bfloat16)).reshape(k // 32, 32, n)
    amax = np.abs(w).max(1)
    if fmt == "e4m3":
        byte = np.frexp(amax)[1] - 1 + 127 - 7
    else:
        mant, ex = np.frexp(amax / 6.0)
        byte = np.where(mant > 0.5, ex, ex - 1) + 127
    byte = np.clip(np.where(amax > 0, byte, 1), 1, 254)
    scaled = (w * np.exp2(127.0 - byte)[:, None, :]).reshape(k, n).astype(np.float32)
    by_word = np.ascontiguousarray(scaled.reshape(k // 512, 128, 4, n).transpose(0, 1, 3, 2))
    if fmt == "e4m3":
        words = by_word.astype(ml_dtypes.float8_e4m3fn).view(np.uint8)
    else:
        c = by_word.astype(ml_dtypes.float4_e2m1fn).view(np.uint8) & 0xF
        words = (c[..., 0::2] | (c[..., 1::2] << 4)).reshape(k // 512, 128, 2 * n)
    return np.ascontiguousarray(words), np.ascontiguousarray(byte.astype(np.uint8).reshape(k // 512, 16, n))


def unpack_weight(words, scales, fmt):
    g, _, n = scales.shape
    words = np.ascontiguousarray(words).reshape(g, 128, n, -1)
    if fmt == "e4m3":
        vals = words.view(ml_dtypes.float8_e4m3fn).astype(np.float64)
    else:
        nib = np.empty((g, 128, n, 4), np.uint8)
        nib[..., 0::2] = words & 0xF
        nib[..., 1::2] = words >> 4
        vals = E2M1[nib]
    vals = vals * np.repeat(np.exp2(scales.astype(np.float64) - 127.0), 8, axis=1)[..., None]
    return vals.transpose(0, 1, 3, 2).reshape(g * 512, n)


D, K, T, U, I, Q = 512, 512, 1024, 1024, 512, 128


def setup_inputs():
    n = np.random.standard_normal
    idx = np.stack([np.random.permutation(T)[:I] for _ in range(8)])
    idx2 = np.stack([np.random.permutation(U)[:I] for _ in range(8)])
    idx3 = np.stack([np.random.permutation(T)[:I] for _ in range(8)])
    idx4 = np.stack([np.random.permutation(T)[:I] for _ in range(8)])
    idx5 = np.stack([np.random.permutation(U)[:I] for _ in range(8)])
    idx6 = np.stack([np.random.permutation(T)[:I] for _ in range(8)])
    fd = mx_kscale(D)
    fk = mx_kscale(K)
    wqp = pack_weight(n((D, K)) * 1.0 / np.sqrt(D) * fd[:, None] * fk, "e4m3")
    keysp = pack_weight(n((K, T)) * 1.0 / np.sqrt(K) / fk[:, None], "e2m1")
    notesp = pack_weight(n((D, U)) * 1.0 / np.sqrt(D) * fd[:, None], "e4m3")
    return {
        "states": (n((D, Q)) * 0.95 / fd[:, None]).astype(np.float32),
        "wq_words": wqp[0],
        "wq_scales": wqp[1],
        "keys_words": keysp[0],
        "keys_scales": keysp[1],
        "notes_words": notesp[0],
        "notes_scales": notesp[1],
        "offs": striped8(idx),
        "offs2": striped8(idx2),
        "offs3": striped8(idx3),
        "offs4": striped8(idx4),
        "offs5": striped8(idx5),
        "offs6": striped8(idx6),
    }


def reference(states, wq_words, wq_scales, keys_words, keys_scales, notes_words, notes_scales, offs, offs2, offs3, offs4, offs5, offs6):
    idx = unstriped8(offs)
    idx2 = unstriped8(offs2)
    idx3 = unstriped8(offs3)
    idx4 = unstriped8(offs4)
    idx5 = unstriped8(offs5)
    idx6 = unstriped8(offs6)
    wqu = unpack_weight(wq_words, wq_scales, "e4m3")
    keysu = unpack_weight(keys_words, keys_scales, "e2m1")
    notesu = unpack_weight(notes_words, notes_scales, "e4m3")
    statesq = mxq(f64(states), 0, "e4m3")
    qv = wqu.T @ statesq
    qvq = mxq(qv, 0, "e4m3")
    a = qvq.T @ keysu
    b = statesq.T @ notesu
    r = pick8(b, idx2, 16) - pick8(a, idx, 16)
    f1 = np.zeros((Q, T))
    f1[np.arange(Q)[:, None], idx[np.arange(Q) % 128 // 16]] = r
    a2 = a + f1
    v = np.maximum(pick8(a2, idx3, 16), pick8(b, idx5, 16))
    f2 = np.zeros((Q, T))
    f2[np.arange(Q)[:, None], idx4[np.arange(Q) % 128 // 16]] = v
    a3 = a2 + f2
    y = pick8(a3, idx6, 16)
    return y

@@ -1,0 +1,163 @@
+from contextlib import ExitStack
+
+import concourse.mybir as mybir
+
+D, K, T, U, I, Q = 512, 512, 1024, 1024, 512, 128
+FLOPS = 2 * (D * K * Q + K * Q * T + D * Q * U)
+
+F32 = mybir.dt.float32
+BF16 = mybir.dt.bfloat16
+I32 = mybir.dt.int32
+U32 = mybir.dt.uint32
+U16 = mybir.dt.uint16
+U8 = mybir.dt.uint8
+E4M3 = mybir.dt.float8_e4m3fn_x4
+E2M1 = mybir.dt.float4_e2m1fn_x4
+ALU = mybir.AluOpType
+COPY = mybir.ActivationFunctionType.Copy
+
+P = 128
+PACK = 4
+HALF = I // 2
+LIST_ROWS = 16
+B_COLS = 512
+A_COLS = 256
+
+
+def tile_attend_mendedtwice_madeside_kernel(tc, states, wq_words, wq_scales, keys_words, keys_scales,
+                                             notes_words, notes_scales, offs, offs2, offs3, offs4, offs5,
+                                             offs6, out):
+    nc = tc.nc
+    with ExitStack() as ctx:
+        lists = ctx.enter_context(tc.tile_pool(name="lists", bufs=1))
+        sb = ctx.enter_context(tc.tile_pool(name="sb", bufs=1))
+        psum = ctx.enter_context(tc.psum_pool(name="psum", bufs=1))
+
+        def zeroed_plane(name, width):
+            plane = sb.tile([P, width], U8, name=name, align_bytes=64)
+            nc.vector.memset(plane[:].bitcast(I32), 0)
+            return plane
+
+        def load_scale_rows(plane, scales):
+            for quad in range(4):
+                nc.sync.dma_start(out=plane[32 * quad : 32 * quad + 4, :].bitcast(I32),
+                                  in_=scales[0, 4 * quad : 4 * quad + 4, :].bitcast(I32))
+
+        def load_list(name, src):
+            held = lists.tile([P, I // LIST_ROWS], U16, name=name)
+            nc.sync.dma_start(held[:], src)
+            return held
+
+        def half(held, h):
+            cols = HALF // LIST_ROWS
+            return held[:, h * cols : (h + 1) * cols]
+
+        def slots(h):
+            return slice(h * HALF, (h + 1) * HALF)
+
+        wq_plane_raw = zeroed_plane("wq_plane_raw", K)
+        notes_plane = zeroed_plane("notes_plane", U)
+        keys_plane = zeroed_plane("keys_plane", T)
+        f1 = sb.tile([P, T], F32, name="f1")
+        f2 = sb.tile([P, T], F32, name="f2")
+        nc.vector.memset(f1[:], 0.0)
+        nc.vector.memset(f2[:], 0.0)
+
+        states_raw = sb.tile([P, PACK, Q], F32, name="states_raw")
+        nc.sync.dma_start(out=states_raw[:], in_=states.rearrange("(p j) q -> p j q", j=PACK))
+        load_scale_rows(wq_plane_raw, wq_scales)
+        wq_raw = sb.tile([P, K], U32, name="wq_raw", align_bytes=64)
+        nc.sync.dma_start(out=wq_raw[:].bitcast(I32),
+                          in_=wq_words[0].rearrange("p c r -> p (c r)").bitcast(I32))
+        load_scale_rows(notes_plane, notes_scales)
+        notes_codes = sb.tile([P, U], U32, name="notes_codes", align_bytes=64)
+        nc.sync.dma_start(out=notes_codes[:].bitcast(I32),
+                          in_=notes_words[0].rearrange("p c r -> p (c r)").bitcast(I32))
+        load_scale_rows(keys_plane, keys_scales)
+        keys_codes = sb.tile([P, 2 * T], U8, name="keys_codes", align_bytes=64)
+        nc.sync.dma_start(out=keys_codes[:].bitcast(I32), in_=keys_words[0].bitcast(I32))
+        idx2 = load_list("idx2", offs2)
+        idx = load_list("idx", offs)
+        idx5 = load_list("idx5", offs5)
+        idx3 = load_list("idx3", offs3)
+        idx4 = load_list("idx4", offs4)
+        idx6 = load_list("idx6", offs6)
+
+        states_bf = sb.tile([P, Q, PACK], BF16, name="states_bf", align_bytes=64)
+        nc.scalar.activation(states_bf[:].rearrange("p (c i) j -> p c j i", i=4),
+                             states_raw[:].rearrange("p j (c i) -> p c j i", i=4), COPY)
+
+        wq_plane = sb.tile([P, PACK, P], U8, name="wq_plane", align_bytes=64)
+        nc.vector.tensor_copy(wq_plane[:], wq_plane_raw[:].rearrange("p (m t) -> p t m", t=PACK))
+        wq_codes = sb.tile([P, PACK, P], U32, name="wq_codes", align_bytes=64)
+        nc.vector.tensor_copy(wq_codes[:].rearrange("p t (c i) -> p c t i", i=4),
+                              wq_raw[:].rearrange("p (c i t) -> p c t i", i=4, t=PACK))
+
+        states_codes = sb.tile([P, Q], U32, name="states_codes", align_bytes=64)
+        states_plane = sb.tile([P, Q], U8, name="states_plane", align_bytes=64)
+        nc.vector.quantize_mx(out=states_codes[:].bitcast(E4M3), scales=states_plane[:],
+                              in_=states_bf[:].rearrange("p q j -> p (q j)"))
+
+        qv_ps = psum.tile([P, PACK, Q], F32, name="qv_ps")
+        for t in range(PACK):
+            nc.tensor.matmul_mx(out=qv_ps[:, t, :], lhsT=wq_codes[:, t, :].bitcast(E4M3),
+                                lhsT_scale=wq_plane[:, t, :], rhs=states_codes[:].bitcast(E4M3),
+                                rhs_scale=states_plane[:], start=True, stop=True)
+
+        b = sb.tile([P, U], F32, name="b")
+        for n in range(U // B_COLS):
+            cols = slice(n * B_COLS, (n + 1) * B_COLS)
+            b_ps = psum.tile([P, B_COLS], F32, name="b_ps%d" % n)
+            nc.tensor.matmul_mx(out=b_ps[:], lhsT=states_codes[:].bitcast(E4M3), lhsT_scale=states_plane[:],
+                                rhs=notes_codes[:, cols].bitcast(E4M3), rhs_scale=notes_plane[:, cols],
+                                start=True, stop=True)
+            nc.scalar.copy(b[:, cols], b_ps[:])
+
+        qv_bf = sb.tile([P, Q, PACK], BF16, name="qv_bf", align_bytes=64)
+        nc.vector.tensor_copy(qv_bf[:], qv_ps[:].rearrange("p t q -> p q t"))
+        qv_codes = sb.tile([P, Q], U32, name="qv_codes", align_bytes=64)
+        qv_plane = sb.tile([P, Q], U8, name="qv_plane", align_bytes=64)
+        nc.vector.quantize_mx(out=qv_codes[:].bitcast(E4M3), scales=qv_plane[:],
+                              in_=qv_bf[:].rearrange("p q t -> p (q t)"))
+
+        a = sb.tile([P, T], F32, name="a")
+        for n in range(T // A_COLS):
+            cols = slice(n * A_COLS, (n + 1) * A_COLS)
+            a_ps = psum.tile([P, A_COLS], F32, name="a_ps%d" % n)
+            nc.tensor.matmul_mx(out=a_ps[:], lhsT=qv_codes[:].bitcast(E4M3), lhsT_scale=qv_plane[:],
+                                rhs=keys_codes[:, 2 * n * A_COLS : 2 * (n + 1) * A_COLS].bitcast(E2M1),
+                                rhs_scale=keys_plane[:, cols], start=True, stop=True)
+            if n < T // A_COLS - 1:
+                nc.vector.tensor_copy(a[:, cols], a_ps[:])
+            else:
+                nc.scalar.copy(a[:, cols], a_ps[:])
+
+        b_at2 = sb.tile([P, I], F32, name="b_at2")
+        neg_a = sb.tile([P, I], F32, name="neg_a")
+        nc.scalar.activation(b_at2[:, slots(0)], b[:].indirect(half(idx2, 0)), COPY)
+        nc.vector.tensor_scalar(neg_a[:, slots(0)], a[:].indirect(half(idx, 0)), -1.0, 0.0, ALU.mult, ALU.add)
+        nc.scalar.activation(neg_a[:, slots(1)], a[:].indirect(half(idx, 1)), COPY, scale=-1.0)
+        nc.scalar.activation(b_at2[:, slots(1)], b[:].indirect(half(idx2, 1)), COPY)
+        for h in range(2):
+            nc.vector.tensor_tensor(f1[:].indirect(half(idx, h)), b_at2[:, slots(h)], neg_a[:, slots(h)], ALU.add)
+        b_at5 = sb.tile([P, I], F32, name="b_at5")
+        nc.scalar.activation(b_at5[:], b[:].indirect(idx5[:]), COPY)
+
+        a2 = sb.tile([P, T], F32, name="a2")
+        nc.vector.tensor_tensor(a2[:], a[:], f1[:], ALU.add)
+
+        a2_at3 = sb.tile([P, I], F32, name="a2_at3")
+        v = sb.tile([P, I], F32, name="v")
+        nc.vector.tensor_copy(a2_at3[:, slots(0)], a2[:].indirect(half(idx3, 0)))
+        nc.scalar.activation(a2_at3[:, slots(1)], a2[:].indirect(half(idx3, 1)), COPY)
+        nc.vector.tensor_tensor(v[:], a2_at3[:], b_at5[:], ALU.max)
+        nc.vector.tensor_copy(f2[:].indirect(idx4[:]), v[:])
+
+        a3 = sb.tile([P, T], F32, name="a3")
+        nc.vector.tensor_tensor(a3[:], a2[:], f2[:], ALU.add)
+
+        y = sb.tile([P, I], F32, name="y")
+        nc.vector.tensor_copy(y[:, slots(0)], a3[:].indirect(half(idx6, 0)))
+        nc.scalar.activation(y[:, slots(1)], a3[:].indirect(half(idx6, 1)), COPY)
+        nc.sync.dma_start(out=out[:, slots(0)], in_=y[:, slots(0)])
+        nc.scalar.dma_start(out=out[:, slots(1)], in_=y[:, slots(1)])

@@ -58,10 +58,6 @@ def tile_attend_mendedtwice_madeside_kernel(tc, states, wq_words, wq_scales, key
         wq_plane_raw = zeroed_plane("wq_plane_raw", K)
         notes_plane = zeroed_plane("notes_plane", U)
         keys_plane = zeroed_plane("keys_plane", T)
-        f1 = sb.tile([P, T], F32, name="f1")
-        f2 = sb.tile([P, T], F32, name="f2")
-        nc.vector.memset(f1[:], 0.0)
-        nc.vector.memset(f2[:], 0.0)
 
         states_raw = sb.tile([P, PACK, Q], F32, name="states_raw")
         nc.sync.dma_start(out=states_raw[:], in_=states.rearrange("(p j) q -> p j q", j=PACK))
@@ -71,11 +67,11 @@ def tile_attend_mendedtwice_madeside_kernel(tc, states, wq_words, wq_scales, key
                           in_=wq_words[0].rearrange("p c r -> p (c r)").bitcast(I32))
         load_scale_rows(notes_plane, notes_scales)
         notes_codes = sb.tile([P, U], U32, name="notes_codes", align_bytes=64)
-        nc.sync.dma_start(out=notes_codes[:].bitcast(I32),
+        nc.gpsimd.dma_start(out=notes_codes[:].bitcast(I32),
                           in_=notes_words[0].rearrange("p c r -> p (c r)").bitcast(I32))
         load_scale_rows(keys_plane, keys_scales)
-        keys_codes = sb.tile([P, 2 * T], U8, name="keys_codes", align_bytes=64)
-        nc.sync.dma_start(out=keys_codes[:].bitcast(I32), in_=keys_words[0].bitcast(I32))
+        keys_codes = sb.tile([P, 2 * T], U8, name="keys_codes", tag="keys_then_b2", align_bytes=64)
+        nc.gpsimd.dma_start(out=keys_codes[:].bitcast(I32), in_=keys_words[0].bitcast(I32))
         idx2 = load_list("idx2", offs2)
         idx = load_list("idx", offs)
         idx5 = load_list("idx5", offs5)
@@ -83,7 +79,7 @@ def tile_attend_mendedtwice_madeside_kernel(tc, states, wq_words, wq_scales, key
         idx4 = load_list("idx4", offs4)
         idx6 = load_list("idx6", offs6)
 
-        states_bf = sb.tile([P, Q, PACK], BF16, name="states_bf", align_bytes=64)
+        states_bf = sb.tile([P, Q, PACK], BF16, name="states_bf", tag="first_mend", align_bytes=64)
         nc.scalar.activation(states_bf[:].rearrange("p (c i) j -> p c j i", i=4),
                              states_raw[:].rearrange("p j (c i) -> p c j i", i=4), COPY)
 
@@ -97,6 +93,9 @@ def tile_attend_mendedtwice_madeside_kernel(tc, states, wq_words, wq_scales, key
         states_plane = sb.tile([P, Q], U8, name="states_plane", align_bytes=64)
         nc.vector.quantize_mx(out=states_codes[:].bitcast(E4M3), scales=states_plane[:],
                               in_=states_bf[:].rearrange("p q j -> p (q j)"))
+
+        f1 = sb.tile([P, T], F32, name="f1", tag="first_mend", align_bytes=64)
+        nc.gpsimd.memset(f1[:], 0.0)
 
         qv_ps = psum.tile([P, PACK, Q], F32, name="qv_ps")
         for t in range(PACK):
@@ -113,12 +112,15 @@ def tile_attend_mendedtwice_madeside_kernel(tc, states, wq_words, wq_scales, key
                                 start=True, stop=True)
             nc.scalar.copy(b[:, cols], b_ps[:])
 
-        qv_bf = sb.tile([P, Q, PACK], BF16, name="qv_bf", align_bytes=64)
+        qv_bf = sb.tile([P, Q, PACK], BF16, name="qv_bf", tag="second_mend", align_bytes=64)
         nc.vector.tensor_copy(qv_bf[:], qv_ps[:].rearrange("p t q -> p q t"))
-        qv_codes = sb.tile([P, Q], U32, name="qv_codes", align_bytes=64)
+        qv_codes = sb.tile([P, Q], U32, name="qv_codes", tag="qv_then_b5", align_bytes=64)
         qv_plane = sb.tile([P, Q], U8, name="qv_plane", align_bytes=64)
         nc.vector.quantize_mx(out=qv_codes[:].bitcast(E4M3), scales=qv_plane[:],
                               in_=qv_bf[:].rearrange("p q t -> p (q t)"))
+
+        f2 = sb.tile([P, T], F32, name="f2", tag="second_mend", align_bytes=64)
+        nc.gpsimd.memset(f2[:], 0.0)
 
         a = sb.tile([P, T], F32, name="a")
         for n in range(T // A_COLS):
@@ -127,12 +129,12 @@ def tile_attend_mendedtwice_madeside_kernel(tc, states, wq_words, wq_scales, key
             nc.tensor.matmul_mx(out=a_ps[:], lhsT=qv_codes[:].bitcast(E4M3), lhsT_scale=qv_plane[:],
                                 rhs=keys_codes[:, 2 * n * A_COLS : 2 * (n + 1) * A_COLS].bitcast(E2M1),
                                 rhs_scale=keys_plane[:, cols], start=True, stop=True)
-            if n < T // A_COLS - 1:
+            if n % 2 == 0:
                 nc.vector.tensor_copy(a[:, cols], a_ps[:])
             else:
                 nc.scalar.copy(a[:, cols], a_ps[:])
 
-        b_at2 = sb.tile([P, I], F32, name="b_at2")
+        b_at2 = sb.tile([P, I], F32, name="b_at2", tag="keys_then_b2", align_bytes=64)
         neg_a = sb.tile([P, I], F32, name="neg_a")
         nc.scalar.activation(b_at2[:, slots(0)], b[:].indirect(half(idx2, 0)), COPY)
         nc.vector.tensor_scalar(neg_a[:, slots(0)], a[:].indirect(half(idx, 0)), -1.0, 0.0, ALU.mult, ALU.add)
@@ -140,7 +142,7 @@ def tile_attend_mendedtwice_madeside_kernel(tc, states, wq_words, wq_scales, key
         nc.scalar.activation(b_at2[:, slots(1)], b[:].indirect(half(idx2, 1)), COPY)
         for h in range(2):
             nc.vector.tensor_tensor(f1[:].indirect(half(idx, h)), b_at2[:, slots(h)], neg_a[:, slots(h)], ALU.add)
-        b_at5 = sb.tile([P, I], F32, name="b_at5")
+        b_at5 = sb.tile([P, I], F32, name="b_at5", tag="qv_then_b5", align_bytes=64)
         nc.scalar.activation(b_at5[:], b[:].indirect(idx5[:]), COPY)
 
         a2 = sb.tile([P, T], F32, name="a2")
@@ -150,7 +152,8 @@ def tile_attend_mendedtwice_madeside_kernel(tc, states, wq_words, wq_scales, key
         v = sb.tile([P, I], F32, name="v")
         nc.vector.tensor_copy(a2_at3[:, slots(0)], a2[:].indirect(half(idx3, 0)))
         nc.scalar.activation(a2_at3[:, slots(1)], a2[:].indirect(half(idx3, 1)), COPY)
-        nc.vector.tensor_tensor(v[:], a2_at3[:], b_at5[:], ALU.max)
+        for h in (1, 0):
+            nc.vector.tensor_tensor(v[:, slots(h)], a2_at3[:, slots(h)], b_at5[:, slots(h)], ALU.max)
         nc.vector.tensor_copy(f2[:].indirect(idx4[:]), v[:])
 
         a3 = sb.tile([P, T], F32, name="a3")

@@ -80,19 +80,22 @@ def tile_attend_mendedtwice_madeside_kernel(tc, states, wq_words, wq_scales, key
         idx6 = load_list("idx6", offs6)
 
         states_bf = sb.tile([P, Q, PACK], BF16, name="states_bf", tag="first_mend", align_bytes=64)
-        nc.scalar.activation(states_bf[:].rearrange("p (c i) j -> p c j i", i=4),
-                             states_raw[:].rearrange("p j (c i) -> p c j i", i=4), COPY)
+        nc.vector.tensor_copy(states_bf[:].rearrange("p (c i) j -> p c j i", i=4),
+                              states_raw[:].rearrange("p j (c i) -> p c j i", i=4))
 
         wq_plane = sb.tile([P, PACK, P], U8, name="wq_plane", align_bytes=64)
         nc.vector.tensor_copy(wq_plane[:], wq_plane_raw[:].rearrange("p (m t) -> p t m", t=PACK))
         wq_codes = sb.tile([P, PACK, P], U32, name="wq_codes", align_bytes=64)
-        nc.vector.tensor_copy(wq_codes[:].rearrange("p t (c i) -> p c t i", i=4),
-                              wq_raw[:].rearrange("p (c i t) -> p c t i", i=4, t=PACK))
 
         states_codes = sb.tile([P, Q], U32, name="states_codes", align_bytes=64)
         states_plane = sb.tile([P, Q], U8, name="states_plane", align_bytes=64)
         nc.vector.quantize_mx(out=states_codes[:].bitcast(E4M3), scales=states_plane[:],
                               in_=states_bf[:].rearrange("p q j -> p (q j)"))
+
+        dealt = wq_codes[:].rearrange("p t (c i) -> p c t i", i=4)
+        as_loaded = wq_raw[:].rearrange("p (c i t) -> p c t i", i=4, t=PACK)
+        nc.vector.tensor_copy(dealt[:, :, 0:2, :], as_loaded[:, :, 0:2, :])
+        nc.scalar.copy(dealt[:, :, 2:4, :], as_loaded[:, :, 2:4, :])
 
         f1 = sb.tile([P, T], F32, name="f1", tag="first_mend", align_bytes=64)
         nc.gpsimd.memset(f1[:], 0.0)
@@ -123,12 +126,14 @@ def tile_attend_mendedtwice_madeside_kernel(tc, states, wq_words, wq_scales, key
         nc.gpsimd.memset(f2[:], 0.0)
 
         a = sb.tile([P, T], F32, name="a")
+        a_banks = []
         for n in range(T // A_COLS):
             cols = slice(n * A_COLS, (n + 1) * A_COLS)
             a_ps = psum.tile([P, A_COLS], F32, name="a_ps%d" % n)
             nc.tensor.matmul_mx(out=a_ps[:], lhsT=qv_codes[:].bitcast(E4M3), lhsT_scale=qv_plane[:],
                                 rhs=keys_codes[:, 2 * n * A_COLS : 2 * (n + 1) * A_COLS].bitcast(E2M1),
                                 rhs_scale=keys_plane[:, cols], start=True, stop=True)
+            a_banks.append(a_ps)
             if n % 2 == 0:
                 nc.vector.tensor_copy(a[:, cols], a_ps[:])
             else:
@@ -146,7 +151,11 @@ def tile_attend_mendedtwice_madeside_kernel(tc, states, wq_words, wq_scales, key
         nc.scalar.activation(b_at5[:], b[:].indirect(idx5[:]), COPY)
 
         a2 = sb.tile([P, T], F32, name="a2")
-        nc.vector.tensor_tensor(a2[:], a[:], f1[:], ALU.add)
+        for n in range(T // A_COLS - 1):
+            cols = slice(n * A_COLS, (n + 1) * A_COLS)
+            nc.vector.tensor_tensor(a2[:, cols], a_banks[n][:], f1[:, cols], ALU.add)
+        cols = slice(T - A_COLS, T)
+        nc.gpsimd.tensor_tensor(a2[:, cols], a[:, cols], f1[:, cols], ALU.add)
 
         a2_at3 = sb.tile([P, I], F32, name="a2_at3")
         v = sb.tile([P, I], F32, name="v")

@@ -79,7 +79,7 @@ def tile_attend_mendedtwice_madeside_kernel(tc, states, wq_words, wq_scales, key
         idx4 = load_list("idx4", offs4)
         idx6 = load_list("idx6", offs6)
 
-        states_bf = sb.tile([P, Q, PACK], BF16, name="states_bf", tag="first_mend", align_bytes=64)
+        states_bf = sb.tile([P, Q, PACK], BF16, name="states_bf", align_bytes=64)
         nc.vector.tensor_copy(states_bf[:].rearrange("p (c i) j -> p c j i", i=4),
                               states_raw[:].rearrange("p j (c i) -> p c j i", i=4))
 
@@ -97,9 +97,6 @@ def tile_attend_mendedtwice_madeside_kernel(tc, states, wq_words, wq_scales, key
         nc.vector.tensor_copy(dealt[:, :, 0:2, :], as_loaded[:, :, 0:2, :])
         nc.scalar.copy(dealt[:, :, 2:4, :], as_loaded[:, :, 2:4, :])
 
-        f1 = sb.tile([P, T], F32, name="f1", tag="first_mend", align_bytes=64)
-        nc.gpsimd.memset(f1[:], 0.0)
-
         qv_ps = psum.tile([P, PACK, Q], F32, name="qv_ps")
         for t in range(PACK):
             nc.tensor.matmul_mx(out=qv_ps[:, t, :], lhsT=wq_codes[:, t, :].bitcast(E4M3),
@@ -115,15 +112,15 @@ def tile_attend_mendedtwice_madeside_kernel(tc, states, wq_words, wq_scales, key
                                 start=True, stop=True)
             nc.scalar.copy(b[:, cols], b_ps[:])
 
-        qv_bf = sb.tile([P, Q, PACK], BF16, name="qv_bf", tag="second_mend", align_bytes=64)
+        qv_bf = sb.tile([P, Q, PACK], BF16, name="qv_bf", tag="qv_then_f1", align_bytes=64)
         nc.vector.tensor_copy(qv_bf[:], qv_ps[:].rearrange("p t q -> p q t"))
         qv_codes = sb.tile([P, Q], U32, name="qv_codes", tag="qv_then_b5", align_bytes=64)
         qv_plane = sb.tile([P, Q], U8, name="qv_plane", align_bytes=64)
         nc.vector.quantize_mx(out=qv_codes[:].bitcast(E4M3), scales=qv_plane[:],
                               in_=qv_bf[:].rearrange("p q t -> p (q t)"))
 
-        f2 = sb.tile([P, T], F32, name="f2", tag="second_mend", align_bytes=64)
-        nc.gpsimd.memset(f2[:], 0.0)
+        f1 = sb.tile([P, T], F32, name="f1", tag="qv_then_f1", align_bytes=64)
+        nc.gpsimd.memset(f1[:], 0.0)
 
         a = sb.tile([P, T], F32, name="a")
         a_banks = []
@@ -140,13 +137,16 @@ def tile_attend_mendedtwice_madeside_kernel(tc, states, wq_words, wq_scales, key
                 nc.scalar.copy(a[:, cols], a_ps[:])
 
         b_at2 = sb.tile([P, I], F32, name="b_at2", tag="keys_then_b2", align_bytes=64)
-        neg_a = sb.tile([P, I], F32, name="neg_a")
+        neg_a = [sb.tile([P, HALF], F32, name="neg_a0", tag="neg_a_then_f2"),
+                 sb.tile([P, HALF], F32, name="neg_a1")]
         nc.scalar.activation(b_at2[:, slots(0)], b[:].indirect(half(idx2, 0)), COPY)
-        nc.vector.tensor_scalar(neg_a[:, slots(0)], a[:].indirect(half(idx, 0)), -1.0, 0.0, ALU.mult, ALU.add)
-        nc.scalar.activation(neg_a[:, slots(1)], a[:].indirect(half(idx, 1)), COPY, scale=-1.0)
+        nc.vector.tensor_scalar(neg_a[0][:], a[:].indirect(half(idx, 0)), -1.0, 0.0, ALU.mult, ALU.add)
+        nc.scalar.activation(neg_a[1][:], a[:].indirect(half(idx, 1)), COPY, scale=-1.0)
         nc.scalar.activation(b_at2[:, slots(1)], b[:].indirect(half(idx2, 1)), COPY)
         for h in range(2):
-            nc.vector.tensor_tensor(f1[:].indirect(half(idx, h)), b_at2[:, slots(h)], neg_a[:, slots(h)], ALU.add)
+            nc.vector.tensor_tensor(f1[:].indirect(half(idx, h)), b_at2[:, slots(h)], neg_a[h][:], ALU.add)
+        f2 = sb.tile([P, T], F32, name="f2", tag="neg_a_then_f2")
+        nc.gpsimd.memset(f2[:], 0.0)
         b_at5 = sb.tile([P, I], F32, name="b_at5", tag="qv_then_b5", align_bytes=64)
         nc.scalar.activation(b_at5[:], b[:].indirect(idx5[:]), COPY)
 

from contextlib import ExitStack

import concourse.mybir as mybir

D, K, T, U, I, Q = 512, 512, 1024, 1024, 512, 128
FLOPS = 2 * (D * K * Q + K * Q * T + D * Q * U)

F32 = mybir.dt.float32
BF16 = mybir.dt.bfloat16
I32 = mybir.dt.int32
U32 = mybir.dt.uint32
U16 = mybir.dt.uint16
U8 = mybir.dt.uint8
E4M3 = mybir.dt.float8_e4m3fn_x4
E2M1 = mybir.dt.float4_e2m1fn_x4
ALU = mybir.AluOpType
COPY = mybir.ActivationFunctionType.Copy

P = 128
PACK = 4
HALF = I // 2
LIST_ROWS = 16
B_COLS = 512
A_COLS = 256


def tile_attend_mendedtwice_madeside_kernel(tc, states, wq_words, wq_scales, keys_words, keys_scales,
                                             notes_words, notes_scales, offs, offs2, offs3, offs4, offs5,
                                             offs6, out):
    nc = tc.nc
    with ExitStack() as ctx:
        lists = ctx.enter_context(tc.tile_pool(name="lists", bufs=1))
        sb = ctx.enter_context(tc.tile_pool(name="sb", bufs=1))
        psum = ctx.enter_context(tc.psum_pool(name="psum", bufs=1))

        def zeroed_plane(name, width):
            plane = sb.tile([P, width], U8, name=name, align_bytes=64)
            nc.vector.memset(plane[:].bitcast(I32), 0)
            return plane

        def load_scale_rows(plane, scales):
            for quad in range(4):
                nc.sync.dma_start(out=plane[32 * quad : 32 * quad + 4, :].bitcast(I32),
                                  in_=scales[0, 4 * quad : 4 * quad + 4, :].bitcast(I32))

        def load_list(name, src):
            held = lists.tile([P, I // LIST_ROWS], U16, name=name)
            nc.sync.dma_start(held[:], src)
            return held

        def half(held, h):
            cols = HALF // LIST_ROWS
            return held[:, h * cols : (h + 1) * cols]

        def slots(h):
            return slice(h * HALF, (h + 1) * HALF)

        wq_plane_raw = zeroed_plane("wq_plane_raw", K)
        notes_plane = zeroed_plane("notes_plane", U)
        keys_plane = zeroed_plane("keys_plane", T)

        states_raw = sb.tile([P, PACK, Q], F32, name="states_raw")
        nc.sync.dma_start(out=states_raw[:], in_=states.rearrange("(p j) q -> p j q", j=PACK))
        load_scale_rows(wq_plane_raw, wq_scales)
        wq_raw = sb.tile([P, K], U32, name="wq_raw", align_bytes=64)
        nc.sync.dma_start(out=wq_raw[:].bitcast(I32),
                          in_=wq_words[0].rearrange("p c r -> p (c r)").bitcast(I32))
        load_scale_rows(notes_plane, notes_scales)
        notes_codes = sb.tile([P, U], U32, name="notes_codes", align_bytes=64)
        nc.gpsimd.dma_start(out=notes_codes[:].bitcast(I32),
                          in_=notes_words[0].rearrange("p c r -> p (c r)").bitcast(I32))
        load_scale_rows(keys_plane, keys_scales)
        keys_codes = sb.tile([P, 2 * T], U8, name="keys_codes", tag="keys_then_b2", align_bytes=64)
        nc.gpsimd.dma_start(out=keys_codes[:].bitcast(I32), in_=keys_words[0].bitcast(I32))
        idx2 = load_list("idx2", offs2)
        idx = load_list("idx", offs)
        idx5 = load_list("idx5", offs5)
        idx3 = load_list("idx3", offs3)
        idx4 = load_list("idx4", offs4)
        idx6 = load_list("idx6", offs6)

        states_bf = sb.tile([P, Q, PACK], BF16, name="states_bf", align_bytes=64)
        nc.vector.tensor_copy(states_bf[:].rearrange("p (c i) j -> p c j i", i=4),
                              states_raw[:].rearrange("p j (c i) -> p c j i", i=4))

        wq_plane = sb.tile([P, PACK, P], U8, name="wq_plane", align_bytes=64)
        nc.vector.tensor_copy(wq_plane[:], wq_plane_raw[:].rearrange("p (m t) -> p t m", t=PACK))
        wq_codes = sb.tile([P, PACK, P], U32, name="wq_codes", align_bytes=64)

        states_codes = sb.tile([P, Q], U32, name="states_codes", align_bytes=64)
        states_plane = sb.tile([P, Q], U8, name="states_plane", align_bytes=64)
        nc.vector.quantize_mx(out=states_codes[:].bitcast(E4M3), scales=states_plane[:],
                              in_=states_bf[:].rearrange("p q j -> p (q j)"))

        dealt = wq_codes[:].rearrange("p t (c i) -> p c t i", i=4)
        as_loaded = wq_raw[:].rearrange("p (c i t) -> p c t i", i=4, t=PACK)
        nc.vector.tensor_copy(dealt[:, :, 0:2, :], as_loaded[:, :, 0:2, :])
        nc.scalar.copy(dealt[:, :, 2:4, :], as_loaded[:, :, 2:4, :])

        qv_ps = psum.tile([P, PACK, Q], F32, name="qv_ps")
        for t in range(PACK):
            nc.tensor.matmul_mx(out=qv_ps[:, t, :], lhsT=wq_codes[:, t, :].bitcast(E4M3),
                                lhsT_scale=wq_plane[:, t, :], rhs=states_codes[:].bitcast(E4M3),
                                rhs_scale=states_plane[:], start=True, stop=True)

        b = sb.tile([P, U], F32, name="b")
        for n in range(U // B_COLS):
            cols = slice(n * B_COLS, (n + 1) * B_COLS)
            b_ps = psum.tile([P, B_COLS], F32, name="b_ps%d" % n)
            nc.tensor.matmul_mx(out=b_ps[:], lhsT=states_codes[:].bitcast(E4M3), lhsT_scale=states_plane[:],
                                rhs=notes_codes[:, cols].bitcast(E4M3), rhs_scale=notes_plane[:, cols],
                                start=True, stop=True)
            nc.scalar.copy(b[:, cols], b_ps[:])

        qv_bf = sb.tile([P, Q, PACK], BF16, name="qv_bf", tag="qv_then_f1", align_bytes=64)
        nc.vector.tensor_copy(qv_bf[:], qv_ps[:].rearrange("p t q -> p q t"))
        qv_codes = sb.tile([P, Q], U32, name="qv_codes", tag="qv_then_b5", align_bytes=64)
        qv_plane = sb.tile([P, Q], U8, name="qv_plane", align_bytes=64)
        nc.vector.quantize_mx(out=qv_codes[:].bitcast(E4M3), scales=qv_plane[:],
                              in_=qv_bf[:].rearrange("p q t -> p (q t)"))

        f1 = sb.tile([P, T], F32, name="f1", tag="qv_then_f1", align_bytes=64)
        nc.gpsimd.memset(f1[:], 0.0)

        a = sb.tile([P, T], F32, name="a")
        a_banks = []
        for n in range(T // A_COLS):
            cols = slice(n * A_COLS, (n + 1) * A_COLS)
            a_ps = psum.tile([P, A_COLS], F32, name="a_ps%d" % n)
            nc.tensor.matmul_mx(out=a_ps[:], lhsT=qv_codes[:].bitcast(E4M3), lhsT_scale=qv_plane[:],
                                rhs=keys_codes[:, 2 * n * A_COLS : 2 * (n + 1) * A_COLS].bitcast(E2M1),
                                rhs_scale=keys_plane[:, cols], start=True, stop=True)
            a_banks.append(a_ps)
            if n % 2 == 0:
                nc.vector.tensor_copy(a[:, cols], a_ps[:])
            else:
                nc.scalar.copy(a[:, cols], a_ps[:])

        b_at2 = sb.tile([P, I], F32, name="b_at2", tag="keys_then_b2", align_bytes=64)
        neg_a = [sb.tile([P, HALF], F32, name="neg_a0", tag="neg_a_then_f2"),
                 sb.tile([P, HALF], F32, name="neg_a1")]
        nc.scalar.activation(b_at2[:, slots(0)], b[:].indirect(half(idx2, 0)), COPY)
        nc.vector.tensor_scalar(neg_a[0][:], a[:].indirect(half(idx, 0)), -1.0, 0.0, ALU.mult, ALU.add)
        nc.scalar.activation(neg_a[1][:], a[:].indirect(half(idx, 1)), COPY, scale=-1.0)
        nc.scalar.activation(b_at2[:, slots(1)], b[:].indirect(half(idx2, 1)), COPY)
        for h in range(2):
            nc.vector.tensor_tensor(f1[:].indirect(half(idx, h)), b_at2[:, slots(h)], neg_a[h][:], ALU.add)
        f2 = sb.tile([P, T], F32, name="f2", tag="neg_a_then_f2")
        nc.gpsimd.memset(f2[:], 0.0)
        b_at5 = sb.tile([P, I], F32, name="b_at5", tag="qv_then_b5", align_bytes=64)
        nc.scalar.activation(b_at5[:], b[:].indirect(idx5[:]), COPY)

        a2 = sb.tile([P, T], F32, name="a2")
        for n in range(T // A_COLS - 1):
            cols = slice(n * A_COLS, (n + 1) * A_COLS)
            nc.vector.tensor_tensor(a2[:, cols], a_banks[n][:], f1[:, cols], ALU.add)
        cols = slice(T - A_COLS, T)
        nc.gpsimd.tensor_tensor(a2[:, cols], a[:, cols], f1[:, cols], ALU.add)

        a2_at3 = sb.tile([P, I], F32, name="a2_at3")
        v = sb.tile([P, I], F32, name="v")
        nc.vector.tensor_copy(a2_at3[:, slots(0)], a2[:].indirect(half(idx3, 0)))
        nc.scalar.activation(a2_at3[:, slots(1)], a2[:].indirect(half(idx3, 1)), COPY)
        for h in (1, 0):
            nc.vector.tensor_tensor(v[:, slots(h)], a2_at3[:, slots(h)], b_at5[:, slots(h)], ALU.max)
        nc.vector.tensor_copy(f2[:].indirect(idx4[:]), v[:])

        a3 = sb.tile([P, T], F32, name="a3")
        nc.vector.tensor_tensor(a3[:], a2[:], f2[:], ALU.add)

        y = sb.tile([P, I], F32, name="y")
        nc.vector.tensor_copy(y[:, slots(0)], a3[:].indirect(half(idx6, 0)))
        nc.scalar.activation(y[:, slots(1)], a3[:].indirect(half(idx6, 1)), COPY)
        nc.sync.dma_start(out=out[:, slots(0)], in_=y[:, slots(0)])
        nc.scalar.dma_start(out=out[:, slots(1)], in_=y[:, slots(1)])
